import numpy as np
import ml_dtypes


def mxq(x, axis, fmt="e4m3"):
    dtype, down = {"e4m3": (ml_dtypes.float8_e4m3fn, 7), "e5m2": (ml_dtypes.float8_e5m2, 14)}[fmt]
    v = np.moveaxis(np.asarray(x, np.float32).astype(ml_dtypes.bfloat16).astype(np.float64), axis, -1)
    blocks = v.reshape(v.shape[:-1] + (-1, 32))
    amax = np.abs(blocks).max(-1, keepdims=True)
    byte = np.maximum(np.where(amax > 0, np.frexp(amax)[1] - 1 + 127, 0) - down, 1)
    scale = np.exp2(byte - 127.0)
    codes = (blocks / scale).astype(np.float32).astype(dtype).astype(np.float64)
    return np.moveaxis((codes * scale).reshape(v.shape), -1, axis)


WIDE = False


def mx_kscale(k):
    if not WIDE:
        return np.ones(k)
    levels = np.array([10, -10, 5, -5, 0])
    if k % 512:
        return np.exp2(np.random.permutation(np.resize(levels, k // 32))).repeat(32)
    a = np.empty((k // 512, 16))
    for p in range(k // 512):
        a[p, :8] = np.random.permutation(np.resize(levels, 8))
        for g in range(8):
            far = levels[np.abs(levels - a[p, g]) >= 10]
            a[p, g + 8] = far[np.random.randint(len(far))]
    return np.exp2(a.ravel()).repeat(32)


def f64(x):
    return np.asarray(x).astype(np.float64)


def striped(idx):
    return np.tile(idx.reshape(-1, 16).T, (8, 1)).astype(np.uint16)


def unstriped(offs):
    return offs[:16].T.reshape(-1).astype(np.int64)


E2M1 = np.array([0.0, 0.5, 1.0, 1.5, 2.0, 3.0, 4.0, 6.0, -0.0, -0.5, -1.0, -1.5, -2.0, -3.0, -4.0, -6.0])


def pack_fp4(w):
    k, n = w.shape
    w = f64(np.asarray(w, np.float32).astype(ml_dtypes.bfloat16)).reshape(k // 32, 32, n)
    amax = np.abs(w).max(1)
    mant, ex = np.frexp(amax / 6.0)
    byte = np.clip(np.where(amax > 0, np.where(mant > 0.5, ex, ex - 1) + 127, 1), 1, 254)
    scaled = (w * np.exp2(127.0 - byte)[:, None, :]).reshape(k, n).astype(np.float32)
    c = np.ascontiguousarray(scaled.reshape(k // 512, 128, 4, n).transpose(0, 1, 3, 2)).astype(ml_dtypes.float4_e2m1fn).view(np.uint8) & 0xF
    words = (c[..., 0::2] | (c[..., 1::2] << 4)).reshape(k // 512, 128, 2 * n)
    return np.ascontiguousarray(words), np.ascontiguousarray(byte.astype(np.uint8).reshape(k // 512, 16, n))


def unpack_fp4(words, scales):
    g, _, n = scales.shape
    words = np.ascontiguousarray(words).reshape(g, 128, n, 2)
    nib = np.empty((g, 128, n, 4), np.uint8)
    nib[..., 0::2] = words & 0xF
    nib[..., 1::2] = words >> 4
    vals = E2M1[nib] * np.repeat(np.exp2(scales.astype(np.float64) - 127.0), 8, axis=1)[..., None]
    return vals.transpose(0, 1, 3, 2).reshape(g * 512, n)


def relu(v):
    return np.maximum(v, 0.0)


K, T, S, N = 1024, 1024, 512, 128


def setup_inputs():
    n = np.random.standard_normal
    s = mx_kscale(K)[:, None]
    packed_w1 = pack_fp4(n((K, N)) / np.sqrt(2 * K) / s)
    packed_w2 = pack_fp4(n((K, N)) / np.sqrt(2 * K) / s)
    return {
        "xT": (n((K, T)) * s).astype(np.float32),
        "w1_words": packed_w1[0],
        "w1_scales": packed_w1[1],
        "w2_words": packed_w2[0],
        "w2_scales": packed_w2[1],
        "offs": striped(np.random.permutation(T)[:S]),
    }


def reference(xT, w1_words, w1_scales, w2_words, w2_scales, offs):
    xq = mxq(f64(xT)[:, unstriped(offs)], 0, "e4m3")
    y0 = unpack_fp4(w1_words, w1_scales).T @ xq
    y1 = unpack_fp4(w2_words, w2_scales).T @ xq
    return relu(y0 + np.pad(y1, ((0, 0), (1, 0)))[:, :S])

@@ -1,0 +1,150 @@
+from contextlib import ExitStack
+
+import concourse.mybir as mybir
+
+K, T, S, M = 1024, 1024, 512, 128
+FLOPS = 2 * 2 * K * S * M
+
+F32 = mybir.dt.float32
+BF16 = mybir.dt.bfloat16
+I32 = mybir.dt.int32
+U32 = mybir.dt.uint32
+U16 = mybir.dt.uint16
+U8 = mybir.dt.uint8
+FP8X4 = mybir.dt.float8_e4m3fn_x4
+FP4X4 = mybir.dt.float4_e2m1fn_x4
+COPY = mybir.ActivationFunctionType.Copy
+RELU = mybir.ActivationFunctionType.Relu
+
+P = 128
+PASSES = 2
+SLICE = 128
+SLICES = S // SLICE
+LIST_COLS = SLICE // 16
+
+CHUNKS = [
+    [(0, 512, 0), (512, 512, 336)],
+    [(0, 512, 0), (512, 512, 336)],
+    [(0, 512, 0), (512, 512, 192)],
+    [(0, 512, 0), (512, 512, 336)],
+]
+
+
+def tile_picked_listconv_relu_e_kernel(
+    tc, xT, w1_words, w1_scales, w2_words, w2_scales, offs, out
+):
+    nc = tc.nc
+    rows = xT.rearrange("(g p u e) t -> g u p e t", g=PASSES, p=P, u=2, e=2)
+
+    with ExitStack() as ctx:
+        keep = ctx.enter_context(tc.tile_pool(name="keep", bufs=1))
+        psum = ctx.enter_context(tc.psum_pool(name="psum", bufs=1))
+
+        offsets = keep.tile([P, S // 16], U16, name="offsets")
+        raw = {}
+        for pair in range(4):
+            for c, (c0, width, vec_cols) in enumerate(CHUNKS[pair]):
+                raw[pair, c] = keep.tile([P, 2, width], F32, name="raw%d_%d" % (pair, c))
+                nc.sync.dma_start(raw[pair, c][:], rows[pair // 2, pair % 2][:, :, c0 : c0 + width])
+                if pair == 0 and c == 0:
+                    nc.sync.dma_start(offsets[:], offs)
+
+        w_words = []
+        w_scales = []
+        for d, (words, scales) in enumerate(((w1_words, w1_scales), (w2_words, w2_scales))):
+            wt = keep.tile([P, PASSES, 2 * M], U8, name="w_words%d" % d, align_bytes=64)
+            nc.sync.dma_start(wt[:].bitcast(I32), words.rearrange("g p b -> p g b").bitcast(I32))
+            st = keep.tile([P, PASSES, M], U8, name="w_scales%d" % d, align_bytes=64)
+            nc.gpsimd.memset(st[:].bitcast(I32), 0)
+            for q in range(4):
+                nc.gpsimd.dma_start(
+                    st[32 * q : 32 * q + 4].bitcast(I32),
+                    scales[:, 4 * q : 4 * q + 4, :].rearrange("g r c -> r g c").bitcast(I32),
+                )
+            w_words.append(wt)
+            w_scales.append(st)
+
+        shifted = keep.tile([P, S], F32, name="shifted")
+        nc.vector.memset(shifted[:, 0:1], 0.0)
+
+        def cast(pair):
+            window = keep.tile([P, T, 2], BF16, name="window%d" % pair)
+            for c, (c0, width, vec_cols) in enumerate(CHUNKS[pair]):
+                src = raw[pair, c][:].rearrange("p e t -> p t e")
+                cut = width - vec_cols
+                nc.scalar.activation(window[:, c0 : c0 + cut, :], src[:, 0:cut, :], COPY)
+                if vec_cols:
+                    nc.vector.tensor_copy(window[:, c0 + cut : c0 + width, :], src[:, cut:width, :])
+            return window[:].rearrange("p t e -> p (t e)").bitcast(U32)
+
+        def gather(picked, window, u, list_cols):
+            words = picked[:].rearrange("p n (u e) -> p (n u e)", u=2).bitcast(U32)
+            nc.vector.tensor_copy(
+                words.rearrange("p (n u) -> p n u", u=2)[:, :, u], window.indirect(offsets[:, list_cols])
+            )
+
+        def quantize(picked, n, name):
+            codes = keep.tile([P, n], U32, name="codes" + name, align_bytes=64)
+            scales = keep.tile([P, n], U8, name="scales" + name, align_bytes=64)
+            nc.vector.quantize_mx(
+                out=codes[:].bitcast(FP8X4), scales=scales[:], in_=picked[:].rearrange("p n j -> p (n j)")
+            )
+            return codes, scales
+
+        acc = {(d, s): psum.tile([P, 512], F32, name="acc%d_%d" % (d, s)) for d in range(2) for s in range(SLICES)}
+
+        def multiply(g, s, codes, scales, taps=(1, 0)):
+            for d in taps:
+                nc.tensor.matmul_mx(
+                    out=acc[d, s][:, 0:SLICE],
+                    lhsT=w_words[d][:, g, :].bitcast(FP4X4),
+                    lhsT_scale=w_scales[d][:, g, :],
+                    rhs=codes.bitcast(FP8X4),
+                    rhs_scale=scales,
+                    start=(g == 0),
+                    stop=(g == PASSES - 1),
+                )
+
+        picked0 = keep.tile([P, S, 4], BF16, name="picked0", align_bytes=64)
+        for u in range(2):
+            gather(picked0, cast(u), u, slice(0, S // 16))
+        window2 = cast(2)
+        codes0, scales0 = quantize(picked0, S, "0")
+        for s in range(SLICES):
+            cols = slice(s * SLICE, (s + 1) * SLICE)
+            multiply(0, s, codes0[:, cols], scales0[:, cols])
+
+        picked1 = [keep.tile([P, SLICE, 4], BF16, name="picked1_%d" % s, align_bytes=64) for s in range(SLICES)]
+        lists = [slice(s * LIST_COLS, (s + 1) * LIST_COLS) for s in range(SLICES)]
+        for s in range(SLICES):
+            gather(picked1[s], window2, 0, lists[s])
+        window3 = cast(3)
+
+        quantized = []
+
+        def product(s):
+            codes, scales = quantize(picked1[s], SLICE, "1_%d" % s)
+            quantized.append((codes, scales))
+            multiply(1, s, codes[:], scales[:], (1,))
+            if s >= 1:
+                multiply(1, s - 1, quantized[s - 1][0][:], quantized[s - 1][1][:], (0,))
+            if s == SLICES - 1:
+                multiply(1, s, codes[:], scales[:], (0,))
+            n = min(SLICE, S - 1 - s * SLICE)
+            nc.scalar.activation(shifted[:, s * SLICE + 1 : s * SLICE + 1 + n], acc[1, s][:, 0:n], COPY)
+
+        def finish(s):
+            cols = slice(s * SLICE, (s + 1) * SLICE)
+            total = keep.tile([P, SLICE], F32, name="total%d" % s)
+            nc.vector.tensor_add(total[:], acc[0, s][:, 0:SLICE], shifted[:, cols])
+            result = keep.tile([P, SLICE], F32, name="result%d" % s)
+            nc.scalar.activation(result[:], total[:], RELU)
+            nc.sync.dma_start(out[:, cols], result[:])
+
+        for s in range(SLICES):
+            gather(picked1[s], window3, 1, lists[s])
+            if s >= 1:
+                product(s - 1)
+        product(SLICES - 1)
+        for s in range(SLICES):
+            finish(s)

@@ -22,12 +22,8 @@ SLICE = 128
 SLICES = S // SLICE
 LIST_COLS = SLICE // 16
 
-CHUNKS = [
-    [(0, 512, 0), (512, 512, 336)],
-    [(0, 512, 0), (512, 512, 336)],
-    [(0, 512, 0), (512, 512, 192)],
-    [(0, 512, 0), (512, 512, 336)],
-]
+HALF = T // 2
+VECTOR_COLS = (336, 336, 0, 336)
 
 
 def tile_picked_listconv_relu_e_kernel(
@@ -41,47 +37,51 @@ def tile_picked_listconv_relu_e_kernel(
         psum = ctx.enter_context(tc.psum_pool(name="psum", bufs=1))
 
         offsets = keep.tile([P, S // 16], U16, name="offsets")
-        raw = {}
-        for pair in range(4):
-            for c, (c0, width, vec_cols) in enumerate(CHUNKS[pair]):
-                raw[pair, c] = keep.tile([P, 2, width], F32, name="raw%d_%d" % (pair, c))
-                nc.sync.dma_start(raw[pair, c][:], rows[pair // 2, pair % 2][:, :, c0 : c0 + width])
-                if pair == 0 and c == 0:
-                    nc.sync.dma_start(offsets[:], offs)
+        w_words = [keep.tile([P, PASSES, 2 * M], U8, name="w_words%d" % d, align_bytes=64) for d in range(2)]
+        w_scales = [keep.tile([P, PASSES, M], U8, name="w_scales%d" % d, align_bytes=64) for d in range(2)]
 
-        w_words = []
-        w_scales = []
-        for d, (words, scales) in enumerate(((w1_words, w1_scales), (w2_words, w2_scales))):
-            wt = keep.tile([P, PASSES, 2 * M], U8, name="w_words%d" % d, align_bytes=64)
-            nc.sync.dma_start(wt[:].bitcast(I32), words.rearrange("g p b -> p g b").bitcast(I32))
-            st = keep.tile([P, PASSES, M], U8, name="w_scales%d" % d, align_bytes=64)
-            nc.gpsimd.memset(st[:].bitcast(I32), 0)
+        raw = []
+
+        def load_x(count):
+            for i in range(len(raw), len(raw) + count):
+                pair, half = divmod(i, 2)
+                raw.append(keep.tile([P, 2, HALF], F32, name="raw%d" % i))
+                nc.sync.dma_start(raw[i][:], rows[pair // 2, pair % 2][:, :, half * HALF : (half + 1) * HALF])
+
+        def load_scales(d, scales):
             for q in range(4):
-                nc.gpsimd.dma_start(
-                    st[32 * q : 32 * q + 4].bitcast(I32),
+                nc.sync.dma_start(
+                    w_scales[d][32 * q : 32 * q + 4].bitcast(I32),
                     scales[:, 4 * q : 4 * q + 4, :].rearrange("g r c -> r g c").bitcast(I32),
                 )
-            w_words.append(wt)
-            w_scales.append(st)
+
+        load_x(3)
+        nc.sync.dma_start(offsets[:], offs)
+        load_scales(1, w2_scales)
+        load_x(3)
+        load_scales(0, w1_scales)
+        load_x(2)
+        for d, words in ((1, w2_words), (0, w1_words)):
+            nc.sync.dma_start(w_words[d][:].bitcast(I32), words.rearrange("g p b -> p g b").bitcast(I32))
 
         shifted = keep.tile([P, S], F32, name="shifted")
         nc.vector.memset(shifted[:, 0:1], 0.0)
 
         def cast(pair):
             window = keep.tile([P, T, 2], BF16, name="window%d" % pair)
-            for c, (c0, width, vec_cols) in enumerate(CHUNKS[pair]):
-                src = raw[pair, c][:].rearrange("p e t -> p t e")
-                cut = width - vec_cols
-                nc.scalar.activation(window[:, c0 : c0 + cut, :], src[:, 0:cut, :], COPY)
-                if vec_cols:
-                    nc.vector.tensor_copy(window[:, c0 + cut : c0 + width, :], src[:, cut:width, :])
+            first, second = [raw[2 * pair + half][:].rearrange("p e t -> p t e") for half in range(2)]
+            cut = HALF - VECTOR_COLS[pair]
+            nc.scalar.activation(window[:, 0:HALF, :], first, COPY)
+            nc.scalar.activation(window[:, HALF : HALF + cut, :], second[:, 0:cut, :], COPY)
+            if cut < HALF:
+                nc.vector.tensor_copy(window[:, HALF + cut : T, :], second[:, cut:HALF, :])
             return window[:].rearrange("p t e -> p (t e)").bitcast(U32)
 
-        def gather(picked, window, u, list_cols):
-            words = picked[:].rearrange("p n (u e) -> p (n u e)", u=2).bitcast(U32)
-            nc.vector.tensor_copy(
-                words.rearrange("p (n u) -> p n u", u=2)[:, :, u], window.indirect(offsets[:, list_cols])
-            )
+        def gather(pairs, window, u, list_cols):
+            nc.vector.tensor_copy(pairs[:, u, :], window.indirect(offsets[:, list_cols]))
+
+        def as_words(picked, dtype):
+            return picked[:].rearrange("p n j -> p (n j)").bitcast(dtype).rearrange("p (n u) -> p n u", u=2)
 
         def quantize(picked, n, name):
             codes = keep.tile([P, n], U32, name="codes" + name, align_bytes=64)
@@ -93,45 +93,47 @@ def tile_picked_listconv_relu_e_kernel(
 
         acc = {(d, s): psum.tile([P, 512], F32, name="acc%d_%d" % (d, s)) for d in range(2) for s in range(SLICES)}
 
-        def multiply(g, s, codes, scales, taps=(1, 0)):
-            for d in taps:
-                nc.tensor.matmul_mx(
-                    out=acc[d, s][:, 0:SLICE],
-                    lhsT=w_words[d][:, g, :].bitcast(FP4X4),
-                    lhsT_scale=w_scales[d][:, g, :],
-                    rhs=codes.bitcast(FP8X4),
-                    rhs_scale=scales,
-                    start=(g == 0),
-                    stop=(g == PASSES - 1),
-                )
+        def multiply(g, d, s, codes, scales):
+            nc.tensor.matmul_mx(
+                out=acc[d, s][:, 0:SLICE],
+                lhsT=w_words[d][:, g, :].bitcast(FP4X4),
+                lhsT_scale=w_scales[d][:, g, :],
+                rhs=codes.bitcast(FP8X4),
+                rhs_scale=scales,
+                start=(g == 0),
+                stop=(g == PASSES - 1),
+            )
 
-        picked0 = keep.tile([P, S, 4], BF16, name="picked0", align_bytes=64)
+        pairs0 = keep.tile([P, 2, S], U32, name="pairs0")
         for u in range(2):
-            gather(picked0, cast(u), u, slice(0, S // 16))
+            gather(pairs0, cast(u), u, slice(0, S // 16))
+        picked0 = keep.tile([P, S, 4], BF16, name="picked0", align_bytes=64)
+        nc.vector.tensor_copy(as_words(picked0, I32), pairs0[:].bitcast(I32).rearrange("p u n -> p n u"))
         window2 = cast(2)
         codes0, scales0 = quantize(picked0, S, "0")
-        for s in range(SLICES):
-            cols = slice(s * SLICE, (s + 1) * SLICE)
-            multiply(0, s, codes0[:, cols], scales0[:, cols])
+        for d in (1, 0):
+            for s in range(SLICES):
+                cols = slice(s * SLICE, (s + 1) * SLICE)
+                multiply(0, d, s, codes0[:, cols], scales0[:, cols])
 
-        picked1 = [keep.tile([P, SLICE, 4], BF16, name="picked1_%d" % s, align_bytes=64) for s in range(SLICES)]
+        pairs1 = [keep.tile([P, 2, SLICE], U32, name="pairs1_%d" % s) for s in range(SLICES)]
         lists = [slice(s * LIST_COLS, (s + 1) * LIST_COLS) for s in range(SLICES)]
         for s in range(SLICES):
-            gather(picked1[s], window2, 0, lists[s])
+            gather(pairs1[s], window2, 0, lists[s])
         window3 = cast(3)
 
         quantized = []
 
-        def product(s):
-            codes, scales = quantize(picked1[s], SLICE, "1_%d" % s)
-            quantized.append((codes, scales))
-            multiply(1, s, codes[:], scales[:], (1,))
-            if s >= 1:
-                multiply(1, s - 1, quantized[s - 1][0][:], quantized[s - 1][1][:], (0,))
-            if s == SLICES - 1:
-                multiply(1, s, codes[:], scales[:], (0,))
+        def tap1(s):
+            picked = keep.tile([P, SLICE, 4], BF16, name="picked1_%d" % s, align_bytes=64)
+            nc.scalar.copy(as_words(picked, U32), pairs1[s][:].rearrange("p u n -> p n u"))
+            quantized.append(quantize(picked, SLICE, "1_%d" % s))
+            multiply(1, 1, s, quantized[s][0][:], quantized[s][1][:])
             n = min(SLICE, S - 1 - s * SLICE)
             nc.scalar.activation(shifted[:, s * SLICE + 1 : s * SLICE + 1 + n], acc[1, s][:, 0:n], COPY)
+
+        def tap0(s):
+            multiply(1, 0, s, quantized[s][0][:], quantized[s][1][:])
 
         def finish(s):
             cols = slice(s * SLICE, (s + 1) * SLICE)
@@ -142,9 +144,11 @@ def tile_picked_listconv_relu_e_kernel(
             nc.sync.dma_start(out[:, cols], result[:])
 
         for s in range(SLICES):
-            gather(picked1[s], window3, 1, lists[s])
+            gather(pairs1[s], window3, 1, lists[s])
+        for s in range(SLICES):
+            tap1(s)
             if s >= 1:
-                product(s - 1)
-        product(SLICES - 1)
+                tap0(s - 1)
+        tap0(SLICES - 1)
         for s in range(SLICES):
             finish(s)

@@ -22,8 +22,8 @@ SLICE = 128
 SLICES = S // SLICE
 LIST_COLS = SLICE // 16
 
-HALF = T // 2
-VECTOR_COLS = (336, 336, 0, 336)
+LOADS = ((1024,), (1024,), (512, 512), (512, 512))
+VECTOR_COLS = (648, 648, 0, 328)
 
 
 def tile_picked_listconv_relu_e_kernel(
@@ -40,45 +40,50 @@ def tile_picked_listconv_relu_e_kernel(
         w_words = [keep.tile([P, PASSES, 2 * M], U8, name="w_words%d" % d, align_bytes=64) for d in range(2)]
         w_scales = [keep.tile([P, PASSES, M], U8, name="w_scales%d" % d, align_bytes=64) for d in range(2)]
 
-        raw = []
+        raw = {}
 
-        def load_x(count):
-            for i in range(len(raw), len(raw) + count):
-                pair, half = divmod(i, 2)
-                raw.append(keep.tile([P, 2, HALF], F32, name="raw%d" % i))
-                nc.sync.dma_start(raw[i][:], rows[pair // 2, pair % 2][:, :, half * HALF : (half + 1) * HALF])
+        def load_x(pair):
+            c0 = 0
+            for i, width in enumerate(LOADS[pair]):
+                raw[pair, i] = keep.tile([P, 2, width], F32, name="raw%d_%d" % (pair, i))
+                nc.sync.dma_start(raw[pair, i][:], rows[pair // 2, pair % 2][:, :, c0 : c0 + width])
+                c0 = c0 + width
 
-        def load_scales(d, scales):
+        def load_scales(queue, d, scales):
             for q in range(4):
-                nc.sync.dma_start(
+                queue.dma_start(
                     w_scales[d][32 * q : 32 * q + 4].bitcast(I32),
                     scales[:, 4 * q : 4 * q + 4, :].rearrange("g r c -> r g c").bitcast(I32),
                 )
 
-        load_x(3)
+        load_x(0)
         nc.sync.dma_start(offsets[:], offs)
-        load_scales(1, w2_scales)
-        load_x(3)
-        load_scales(0, w1_scales)
+        load_x(1)
+        load_scales(nc.sync, 1, w2_scales)
         load_x(2)
+        load_x(3)
         for d, words in ((1, w2_words), (0, w1_words)):
             nc.sync.dma_start(w_words[d][:].bitcast(I32), words.rearrange("g p b -> p g b").bitcast(I32))
+        load_scales(nc.sync, 0, w1_scales)
 
         shifted = keep.tile([P, S], F32, name="shifted")
         nc.vector.memset(shifted[:, 0:1], 0.0)
 
         def cast(pair):
             window = keep.tile([P, T, 2], BF16, name="window%d" % pair)
-            first, second = [raw[2 * pair + half][:].rearrange("p e t -> p t e") for half in range(2)]
-            cut = HALF - VECTOR_COLS[pair]
-            nc.scalar.activation(window[:, 0:HALF, :], first, COPY)
-            nc.scalar.activation(window[:, HALF : HALF + cut, :], second[:, 0:cut, :], COPY)
-            if cut < HALF:
-                nc.vector.tensor_copy(window[:, HALF + cut : T, :], second[:, cut:HALF, :])
+            cut = T - VECTOR_COLS[pair]
+            c0 = 0
+            for i, width in enumerate(LOADS[pair]):
+                src = raw[pair, i][:].rearrange("p e t -> p t e")
+                n = min(width, cut - c0)
+                nc.scalar.activation(window[:, c0 : c0 + n, :], src[:, 0:n, :], COPY)
+                if n < width:
+                    nc.vector.tensor_copy(window[:, c0 + n : c0 + width, :], src[:, n:width, :])
+                c0 = c0 + width
             return window[:].rearrange("p t e -> p (t e)").bitcast(U32)
 
-        def gather(pairs, window, u, list_cols):
-            nc.vector.tensor_copy(pairs[:, u, :], window.indirect(offsets[:, list_cols]))
+        def gather(pairs, window, list_cols):
+            nc.vector.tensor_copy(pairs, window.indirect(offsets[:, list_cols]))
 
         def as_words(picked, dtype):
             return picked[:].rearrange("p n j -> p (n j)").bitcast(dtype).rearrange("p (n u) -> p n u", u=2)
@@ -106,7 +111,7 @@ def tile_picked_listconv_relu_e_kernel(
 
         pairs0 = keep.tile([P, 2, S], U32, name="pairs0")
         for u in range(2):
-            gather(pairs0, cast(u), u, slice(0, S // 16))
+            gather(pairs0[:, u, :], cast(u), slice(0, S // 16))
         picked0 = keep.tile([P, S, 4], BF16, name="picked0", align_bytes=64)
         nc.vector.tensor_copy(as_words(picked0, I32), pairs0[:].bitcast(I32).rearrange("p u n -> p n u"))
         window2 = cast(2)
@@ -116,17 +121,16 @@ def tile_picked_listconv_relu_e_kernel(
                 cols = slice(s * SLICE, (s + 1) * SLICE)
                 multiply(0, d, s, codes0[:, cols], scales0[:, cols])
 
-        pairs1 = [keep.tile([P, 2, SLICE], U32, name="pairs1_%d" % s) for s in range(SLICES)]
+        pairs1 = keep.tile([P, 2, S], U32, name="pairs1")
         lists = [slice(s * LIST_COLS, (s + 1) * LIST_COLS) for s in range(SLICES)]
-        for s in range(SLICES):
-            gather(pairs1[s], window2, 0, lists[s])
+        gather(pairs1[:, 0, :], window2, slice(0, S // 16))
         window3 = cast(3)
 
         quantized = []
 
         def tap1(s):
             picked = keep.tile([P, SLICE, 4], BF16, name="picked1_%d" % s, align_bytes=64)
-            nc.scalar.copy(as_words(picked, U32), pairs1[s][:].rearrange("p u n -> p n u"))
+            nc.scalar.copy(as_words(picked, U32), pairs1[:, :, s * SLICE : (s + 1) * SLICE].rearrange("p u n -> p n u"))
             quantized.append(quantize(picked, SLICE, "1_%d" % s))
             multiply(1, 1, s, quantized[s][0][:], quantized[s][1][:])
             n = min(SLICE, S - 1 - s * SLICE)
@@ -135,20 +139,24 @@ def tile_picked_listconv_relu_e_kernel(
         def tap0(s):
             multiply(1, 0, s, quantized[s][0][:], quantized[s][1][:])
 
-        def finish(s):
-            cols = slice(s * SLICE, (s + 1) * SLICE)
-            total = keep.tile([P, SLICE], F32, name="total%d" % s)
-            nc.vector.tensor_add(total[:], acc[0, s][:, 0:SLICE], shifted[:, cols])
-            result = keep.tile([P, SLICE], F32, name="result%d" % s)
-            nc.scalar.activation(result[:], total[:], RELU)
-            nc.sync.dma_start(out[:, cols], result[:])
+        def add_taps(total, s):
+            nc.vector.tensor_add(total, acc[0, s][:, 0:SLICE], shifted[:, s * SLICE : (s + 1) * SLICE])
 
         for s in range(SLICES):
-            gather(pairs1[s], window3, 1, lists[s])
+            gather(pairs1[:, 1, s * SLICE : (s + 1) * SLICE], window3, lists[s])
         for s in range(SLICES):
             tap1(s)
             if s >= 1:
                 tap0(s - 1)
         tap0(SLICES - 1)
+        total = keep.tile([P, S], F32, name="total")
         for s in range(SLICES):
-            finish(s)
+            add_taps(total[:, s * SLICE : (s + 1) * SLICE], s)
+        first = keep.tile([P, 2 * SLICE], F32, name="result_first")
+        nc.scalar.activation(first[:], total[:, 0 : 2 * SLICE], RELU)
+        nc.sync.dma_start(out[:, 0 : 2 * SLICE], first[:])
+        for s in range(2, SLICES):
+            cols = slice(s * SLICE, (s + 1) * SLICE)
+            result = keep.tile([P, SLICE], F32, name="result%d" % s)
+            nc.vector.tensor_scalar_max(result[:], total[:, cols], 0.0)
+            nc.sync.dma_start(out[:, cols], result[:])

@@ -17,86 +17,93 @@ COPY = mybir.ActivationFunctionType.Copy
 RELU = mybir.ActivationFunctionType.Relu
 
 P = 128
-PASSES = 2
+PASSES = K // (4 * P)
+BANK = 512
+ENTRIES_A_COLUMN = 16
 SLICE = 128
 SLICES = S // SLICE
-LIST_COLS = SLICE // 16
+HALF = S // 2
+RUN = 4
 
-LOADS = ((1024,), (1024,), (512, 512), (512, 512))
-VECTOR_COLS = (648, 648, 0, 328)
+LOAD_WIDTHS = ((512, 512), (512, 256, 256), (512, 512), (512, 512))
+VECTOR_TOKENS = ((0, 320), (0, 256, 160), (0, 128), (0, 320))
 
 
 def tile_picked_listconv_relu_e_kernel(
     tc, xT, w1_words, w1_scales, w2_words, w2_scales, offs, out
 ):
     nc = tc.nc
-    rows = xT.rearrange("(g p u e) t -> g u p e t", g=PASSES, p=P, u=2, e=2)
+    row_pairs = xT.rearrange("(g p u e) c -> g u p e c", g=PASSES, p=P, u=2, e=2)
 
     with ExitStack() as ctx:
         keep = ctx.enter_context(tc.tile_pool(name="keep", bufs=1))
         psum = ctx.enter_context(tc.psum_pool(name="psum", bufs=1))
 
-        offsets = keep.tile([P, S // 16], U16, name="offsets")
+        offsets = keep.tile([P, S // ENTRIES_A_COLUMN], U16, name="offsets")
         w_words = [keep.tile([P, PASSES, 2 * M], U8, name="w_words%d" % d, align_bytes=64) for d in range(2)]
         w_scales = [keep.tile([P, PASSES, M], U8, name="w_scales%d" % d, align_bytes=64) for d in range(2)]
-
         raw = {}
 
-        def load_x(pair):
+        def load_pair(pair):
             c0 = 0
-            for i, width in enumerate(LOADS[pair]):
-                raw[pair, i] = keep.tile([P, 2, width], F32, name="raw%d_%d" % (pair, i))
-                nc.sync.dma_start(raw[pair, i][:], rows[pair // 2, pair % 2][:, :, c0 : c0 + width])
+            for piece, width in enumerate(LOAD_WIDTHS[pair]):
+                raw[pair, piece] = keep.tile([P, 2, width], F32, name="raw%d_%d" % (pair, piece))
+                nc.sync.dma_start(raw[pair, piece][:], row_pairs[pair // 2, pair % 2][:, :, c0 : c0 + width])
                 c0 = c0 + width
 
-        def load_scales(queue, d, scales):
-            for q in range(4):
-                queue.dma_start(
-                    w_scales[d][32 * q : 32 * q + 4].bitcast(I32),
-                    scales[:, 4 * q : 4 * q + 4, :].rearrange("g r c -> r g c").bitcast(I32),
+        def load_scales(d, scale_rows):
+            for quadrant in range(4):
+                nc.sync.dma_start(
+                    w_scales[d][32 * quadrant : 32 * quadrant + 4].bitcast(I32),
+                    scale_rows[:, 4 * quadrant : 4 * quadrant + 4, :].rearrange("g r m -> r g m").bitcast(I32),
                 )
 
-        load_x(0)
+        load_pair(0)
         nc.sync.dma_start(offsets[:], offs)
-        load_x(1)
-        load_scales(nc.sync, 1, w2_scales)
-        load_x(2)
-        load_x(3)
+        load_pair(1)
+        load_scales(1, w2_scales)
+        load_pair(2)
+        load_scales(0, w1_scales)
+        load_pair(3)
         for d, words in ((1, w2_words), (0, w1_words)):
             nc.sync.dma_start(w_words[d][:].bitcast(I32), words.rearrange("g p b -> p g b").bitcast(I32))
-        load_scales(nc.sync, 0, w1_scales)
 
         shifted = keep.tile([P, S], F32, name="shifted")
         nc.vector.memset(shifted[:, 0:1], 0.0)
 
-        def cast(pair):
+        def round_pair(pair):
             window = keep.tile([P, T, 2], BF16, name="window%d" % pair)
-            cut = T - VECTOR_COLS[pair]
             c0 = 0
-            for i, width in enumerate(LOADS[pair]):
-                src = raw[pair, i][:].rearrange("p e t -> p t e")
-                n = min(width, cut - c0)
-                nc.scalar.activation(window[:, c0 : c0 + n, :], src[:, 0:n, :], COPY)
-                if n < width:
-                    nc.vector.tensor_copy(window[:, c0 + n : c0 + width, :], src[:, n:width, :])
+            for piece, width in enumerate(LOAD_WIDTHS[pair]):
+                src = raw[pair, piece][:].rearrange("p e (c i) -> p c e i", i=RUN)
+                dst = window[:, c0 : c0 + width, :].rearrange("p (c i) e -> p c e i", i=RUN)
+                cut = (width - VECTOR_TOKENS[pair][piece]) // RUN
+                if cut > 0:
+                    nc.scalar.activation(dst[:, 0:cut], src[:, 0:cut], COPY)
+                if cut < width // RUN:
+                    nc.vector.tensor_copy(dst[:, cut:], src[:, cut:])
                 c0 = c0 + width
-            return window[:].rearrange("p t e -> p (t e)").bitcast(U32)
+            return window[:].rearrange("p c e -> p (c e)").bitcast(U32)
 
-        def gather(pairs, window, list_cols):
-            nc.vector.tensor_copy(pairs, window.indirect(offsets[:, list_cols]))
+        def gather(gathered, u, window, first, count):
+            columns = slice(first // ENTRIES_A_COLUMN, (first + count) // ENTRIES_A_COLUMN)
+            nc.vector.tensor_copy(gathered[:, u, first : first + count], window.indirect(offsets[:, columns]))
 
-        def as_words(picked, dtype):
-            return picked[:].rearrange("p n j -> p (n j)").bitcast(dtype).rearrange("p (n u) -> p n u", u=2)
+        def weave(copy, dtype, gathered, first, count, name):
+            woven = keep.tile([P, count, 4], BF16, name="woven" + name, align_bytes=64)
+            dst = woven[:].rearrange("p j t -> p (j t)").bitcast(dtype).rearrange("p (c i u) -> p c u i", i=RUN, u=2)
+            copy(dst, gathered[:, :, first : first + count].bitcast(dtype).rearrange("p u (c i) -> p c u i", i=RUN))
+            return woven
 
-        def quantize(picked, n, name):
-            codes = keep.tile([P, n], U32, name="codes" + name, align_bytes=64)
-            scales = keep.tile([P, n], U8, name="scales" + name, align_bytes=64)
+        def quantize(woven, count, name):
+            codes = keep.tile([P, count], U32, name="codes" + name, align_bytes=64)
+            scales = keep.tile([P, count], U8, name="scales" + name, align_bytes=64)
             nc.vector.quantize_mx(
-                out=codes[:].bitcast(FP8X4), scales=scales[:], in_=picked[:].rearrange("p n j -> p (n j)")
+                out=codes[:].bitcast(FP8X4), scales=scales[:], in_=woven[:].rearrange("p j t -> p (j t)")
             )
             return codes, scales
 
-        acc = {(d, s): psum.tile([P, 512], F32, name="acc%d_%d" % (d, s)) for d in range(2) for s in range(SLICES)}
+        acc = {(d, s): psum.tile([P, BANK], F32, name="acc%d_%d" % (d, s)) for d in range(2) for s in range(SLICES)}
 
         def multiply(g, d, s, codes, scales):
             nc.tensor.matmul_mx(
@@ -109,54 +116,47 @@ def tile_picked_listconv_relu_e_kernel(
                 stop=(g == PASSES - 1),
             )
 
-        pairs0 = keep.tile([P, 2, S], U32, name="pairs0")
-        for u in range(2):
-            gather(pairs0[:, u, :], cast(u), slice(0, S // 16))
-        picked0 = keep.tile([P, S, 4], BF16, name="picked0", align_bytes=64)
-        nc.vector.tensor_copy(as_words(picked0, I32), pairs0[:].bitcast(I32).rearrange("p u n -> p n u"))
-        window2 = cast(2)
-        codes0, scales0 = quantize(picked0, S, "0")
+        gathered0 = keep.tile([P, 2, S], U32, name="gathered0")
+        gather(gathered0, 0, round_pair(0), 0, S)
+        window1 = round_pair(1)
+        for h in range(2):
+            gather(gathered0, 1, window1, h * HALF, HALF)
+        woven0 = [weave(nc.vector.tensor_copy, I32, gathered0, h * HALF, HALF, "0_%d" % h) for h in range(2)]
+        window2 = round_pair(2)
+        quantized0 = [quantize(woven0[h], HALF, "0_%d" % h) for h in range(2)]
         for d in (1, 0):
             for s in range(SLICES):
-                cols = slice(s * SLICE, (s + 1) * SLICE)
-                multiply(0, d, s, codes0[:, cols], scales0[:, cols])
+                h, first = divmod(s * SLICE, HALF)
+                codes0, scales0 = quantized0[h]
+                multiply(0, d, s, codes0[:, first : first + SLICE], scales0[:, first : first + SLICE])
 
-        pairs1 = keep.tile([P, 2, S], U32, name="pairs1")
-        lists = [slice(s * LIST_COLS, (s + 1) * LIST_COLS) for s in range(SLICES)]
-        gather(pairs1[:, 0, :], window2, slice(0, S // 16))
-        window3 = cast(3)
-
-        quantized = []
-
-        def tap1(s):
-            picked = keep.tile([P, SLICE, 4], BF16, name="picked1_%d" % s, align_bytes=64)
-            nc.scalar.copy(as_words(picked, U32), pairs1[:, :, s * SLICE : (s + 1) * SLICE].rearrange("p u n -> p n u"))
-            quantized.append(quantize(picked, SLICE, "1_%d" % s))
-            multiply(1, 1, s, quantized[s][0][:], quantized[s][1][:])
-            n = min(SLICE, S - 1 - s * SLICE)
-            nc.scalar.activation(shifted[:, s * SLICE + 1 : s * SLICE + 1 + n], acc[1, s][:, 0:n], COPY)
-
-        def tap0(s):
-            multiply(1, 0, s, quantized[s][0][:], quantized[s][1][:])
-
-        def add_taps(total, s):
-            nc.vector.tensor_add(total, acc[0, s][:, 0:SLICE], shifted[:, s * SLICE : (s + 1) * SLICE])
-
+        gathered1 = keep.tile([P, 2, S], U32, name="gathered1")
+        gather(gathered1, 0, window2, 0, S)
+        window3 = round_pair(3)
         for s in range(SLICES):
-            gather(pairs1[:, 1, s * SLICE : (s + 1) * SLICE], window3, lists[s])
+            gather(gathered1, 1, window3, s * SLICE, SLICE)
+        quantized1 = []
         for s in range(SLICES):
-            tap1(s)
+            woven1 = weave(nc.scalar.copy, U32, gathered1, s * SLICE, SLICE, "1_%d" % s)
+            quantized1.append(quantize(woven1, SLICE, "1_%d" % s))
+            multiply(1, 1, s, quantized1[s][0][:], quantized1[s][1][:])
+            count = min(SLICE, S - 1 - s * SLICE)
+            nc.scalar.copy(shifted[:, s * SLICE + 1 : s * SLICE + 1 + count], acc[1, s][:, 0:count])
             if s >= 1:
-                tap0(s - 1)
-        tap0(SLICES - 1)
+                multiply(1, 0, s - 1, quantized1[s - 1][0][:], quantized1[s - 1][1][:])
+        multiply(1, 0, SLICES - 1, quantized1[SLICES - 1][0][:], quantized1[SLICES - 1][1][:])
+
         total = keep.tile([P, S], F32, name="total")
         for s in range(SLICES):
-            add_taps(total[:, s * SLICE : (s + 1) * SLICE], s)
-        first = keep.tile([P, 2 * SLICE], F32, name="result_first")
-        nc.scalar.activation(first[:], total[:, 0 : 2 * SLICE], RELU)
-        nc.sync.dma_start(out[:, 0 : 2 * SLICE], first[:])
-        for s in range(2, SLICES):
-            cols = slice(s * SLICE, (s + 1) * SLICE)
-            result = keep.tile([P, SLICE], F32, name="result%d" % s)
-            nc.vector.tensor_scalar_max(result[:], total[:, cols], 0.0)
-            nc.sync.dma_start(out[:, cols], result[:])
+            entries = slice(s * SLICE, (s + 1) * SLICE)
+            nc.vector.tensor_add(total[:, entries], acc[0, s][:, 0:SLICE], shifted[:, entries])
+
+        first_half = keep.tile([P, HALF], F32, name="first_half")
+        nc.scalar.activation(first_half[:], total[:, 0:HALF], RELU)
+        nc.sync.dma_start(out[:, 0:HALF], first_half[:])
+        third_slice = keep.tile([P, SLICE], F32, name="third_slice")
+        nc.scalar.activation(third_slice[:], total[:, HALF : HALF + SLICE], RELU)
+        nc.sync.dma_start(out[:, HALF : HALF + SLICE], third_slice[:])
+        last_slice = keep.tile([P, SLICE], F32, name="last_slice")
+        nc.vector.tensor_scalar_max(last_slice[:], total[:, S - SLICE : S], 0.0)
+        nc.sync.dma_start(out[:, S - SLICE : S], last_slice[:])

from contextlib import ExitStack

import concourse.mybir as mybir

K, T, S, M = 1024, 1024, 512, 128
FLOPS = 2 * 2 * K * S * M

F32 = mybir.dt.float32
BF16 = mybir.dt.bfloat16
I32 = mybir.dt.int32
U32 = mybir.dt.uint32
U16 = mybir.dt.uint16
U8 = mybir.dt.uint8
FP8X4 = mybir.dt.float8_e4m3fn_x4
FP4X4 = mybir.dt.float4_e2m1fn_x4
COPY = mybir.ActivationFunctionType.Copy
RELU = mybir.ActivationFunctionType.Relu

P = 128
PASSES = K // (4 * P)
BANK = 512
ENTRIES_A_COLUMN = 16
SLICE = 128
SLICES = S // SLICE
HALF = S // 2
RUN = 4

LOAD_WIDTHS = ((512, 512), (512, 256, 256), (512, 512), (512, 512))
VECTOR_TOKENS = ((0, 320), (0, 256, 160), (0, 128), (0, 320))


def tile_picked_listconv_relu_e_kernel(
    tc, xT, w1_words, w1_scales, w2_words, w2_scales, offs, out
):
    nc = tc.nc
    row_pairs = xT.rearrange("(g p u e) c -> g u p e c", g=PASSES, p=P, u=2, e=2)

    with ExitStack() as ctx:
        keep = ctx.enter_context(tc.tile_pool(name="keep", bufs=1))
        psum = ctx.enter_context(tc.psum_pool(name="psum", bufs=1))

        offsets = keep.tile([P, S // ENTRIES_A_COLUMN], U16, name="offsets")
        w_words = [keep.tile([P, PASSES, 2 * M], U8, name="w_words%d" % d, align_bytes=64) for d in range(2)]
        w_scales = [keep.tile([P, PASSES, M], U8, name="w_scales%d" % d, align_bytes=64) for d in range(2)]
        raw = {}

        def load_pair(pair):
            c0 = 0
            for piece, width in enumerate(LOAD_WIDTHS[pair]):
                raw[pair, piece] = keep.tile([P, 2, width], F32, name="raw%d_%d" % (pair, piece))
                nc.sync.dma_start(raw[pair, piece][:], row_pairs[pair // 2, pair % 2][:, :, c0 : c0 + width])
                c0 = c0 + width

        def load_scales(d, scale_rows):
            for quadrant in range(4):
                nc.sync.dma_start(
                    w_scales[d][32 * quadrant : 32 * quadrant + 4].bitcast(I32),
                    scale_rows[:, 4 * quadrant : 4 * quadrant + 4, :].rearrange("g r m -> r g m").bitcast(I32),
                )

        load_pair(0)
        nc.sync.dma_start(offsets[:], offs)
        load_pair(1)
        load_scales(1, w2_scales)
        load_pair(2)
        load_scales(0, w1_scales)
        load_pair(3)
        for d, words in ((1, w2_words), (0, w1_words)):
            nc.sync.dma_start(w_words[d][:].bitcast(I32), words.rearrange("g p b -> p g b").bitcast(I32))

        shifted = keep.tile([P, S], F32, name="shifted")
        nc.vector.memset(shifted[:, 0:1], 0.0)

        def round_pair(pair):
            window = keep.tile([P, T, 2], BF16, name="window%d" % pair)
            c0 = 0
            for piece, width in enumerate(LOAD_WIDTHS[pair]):
                src = raw[pair, piece][:].rearrange("p e (c i) -> p c e i", i=RUN)
                dst = window[:, c0 : c0 + width, :].rearrange("p (c i) e -> p c e i", i=RUN)
                cut = (width - VECTOR_TOKENS[pair][piece]) // RUN
                if cut > 0:
                    nc.scalar.activation(dst[:, 0:cut], src[:, 0:cut], COPY)
                if cut < width // RUN:
                    nc.vector.tensor_copy(dst[:, cut:], src[:, cut:])
                c0 = c0 + width
            return window[:].rearrange("p c e -> p (c e)").bitcast(U32)

        def gather(gathered, u, window, first, count):
            columns = slice(first // ENTRIES_A_COLUMN, (first + count) // ENTRIES_A_COLUMN)
            nc.vector.tensor_copy(gathered[:, u, first : first + count], window.indirect(offsets[:, columns]))

        def weave(copy, dtype, gathered, first, count, name):
            woven = keep.tile([P, count, 4], BF16, name="woven" + name, align_bytes=64)
            dst = woven[:].rearrange("p j t -> p (j t)").bitcast(dtype).rearrange("p (c i u) -> p c u i", i=RUN, u=2)
            copy(dst, gathered[:, :, first : first + count].bitcast(dtype).rearrange("p u (c i) -> p c u i", i=RUN))
            return woven

        def quantize(woven, count, name):
            codes = keep.tile([P, count], U32, name="codes" + name, align_bytes=64)
            scales = keep.tile([P, count], U8, name="scales" + name, align_bytes=64)
            nc.vector.quantize_mx(
                out=codes[:].bitcast(FP8X4), scales=scales[:], in_=woven[:].rearrange("p j t -> p (j t)")
            )
            return codes, scales

        acc = {(d, s): psum.tile([P, BANK], F32, name="acc%d_%d" % (d, s)) for d in range(2) for s in range(SLICES)}

        def multiply(g, d, s, codes, scales):
            nc.tensor.matmul_mx(
                out=acc[d, s][:, 0:SLICE],
                lhsT=w_words[d][:, g, :].bitcast(FP4X4),
                lhsT_scale=w_scales[d][:, g, :],
                rhs=codes.bitcast(FP8X4),
                rhs_scale=scales,
                start=(g == 0),
                stop=(g == PASSES - 1),
            )

        gathered0 = keep.tile([P, 2, S], U32, name="gathered0")
        gather(gathered0, 0, round_pair(0), 0, S)
        window1 = round_pair(1)
        for h in range(2):
            gather(gathered0, 1, window1, h * HALF, HALF)
        woven0 = [weave(nc.vector.tensor_copy, I32, gathered0, h * HALF, HALF, "0_%d" % h) for h in range(2)]
        window2 = round_pair(2)
        quantized0 = [quantize(woven0[h], HALF, "0_%d" % h) for h in range(2)]
        for d in (1, 0):
            for s in range(SLICES):
                h, first = divmod(s * SLICE, HALF)
                codes0, scales0 = quantized0[h]
                multiply(0, d, s, codes0[:, first : first + SLICE], scales0[:, first : first + SLICE])

        gathered1 = keep.tile([P, 2, S], U32, name="gathered1")
        gather(gathered1, 0, window2, 0, S)
        window3 = round_pair(3)
        for s in range(SLICES):
            gather(gathered1, 1, window3, s * SLICE, SLICE)
        quantized1 = []
        for s in range(SLICES):
            woven1 = weave(nc.scalar.copy, U32, gathered1, s * SLICE, SLICE, "1_%d" % s)
            quantized1.append(quantize(woven1, SLICE, "1_%d" % s))
            multiply(1, 1, s, quantized1[s][0][:], quantized1[s][1][:])
            count = min(SLICE, S - 1 - s * SLICE)
            nc.scalar.copy(shifted[:, s * SLICE + 1 : s * SLICE + 1 + count], acc[1, s][:, 0:count])
            if s >= 1:
                multiply(1, 0, s - 1, quantized1[s - 1][0][:], quantized1[s - 1][1][:])
        multiply(1, 0, SLICES - 1, quantized1[SLICES - 1][0][:], quantized1[SLICES - 1][1][:])

        total = keep.tile([P, S], F32, name="total")
        for s in range(SLICES):
            entries = slice(s * SLICE, (s + 1) * SLICE)
            nc.vector.tensor_add(total[:, entries], acc[0, s][:, 0:SLICE], shifted[:, entries])

        first_half = keep.tile([P, HALF], F32, name="first_half")
        nc.scalar.activation(first_half[:], total[:, 0:HALF], RELU)
        nc.sync.dma_start(out[:, 0:HALF], first_half[:])
        third_slice = keep.tile([P, SLICE], F32, name="third_slice")
        nc.scalar.activation(third_slice[:], total[:, HALF : HALF + SLICE], RELU)
        nc.sync.dma_start(out[:, HALF : HALF + SLICE], third_slice[:])
        last_slice = keep.tile([P, SLICE], F32, name="last_slice")
        nc.vector.tensor_scalar_max(last_slice[:], total[:, S - SLICE : S], 0.0)
        nc.sync.dma_start(out[:, S - SLICE : S], last_slice[:])
